import numpy as np
import ml_dtypes


def mxq(x, axis, fmt="e4m3"):
    dtype, down = {"e4m3": (ml_dtypes.float8_e4m3fn, 7), "e5m2": (ml_dtypes.float8_e5m2, 14)}[fmt]
    v = np.moveaxis(np.asarray(x, np.float32).astype(ml_dtypes.bfloat16).astype(np.float64), axis, -1)
    blocks = v.reshape(v.shape[:-1] + (-1, 32))
    amax = np.abs(blocks).max(-1, keepdims=True)
    byte = np.maximum(np.where(amax > 0, np.frexp(amax)[1] - 1 + 127, 0) - down, 1)
    scale = np.exp2(byte - 127.0)
    codes = (blocks / scale).astype(np.float32).astype(dtype).astype(np.float64)
    return np.moveaxis((codes * scale).reshape(v.shape), -1, axis)


WIDE = False


def mx_kscale(k):
    if not WIDE:
        return np.ones(k)
    levels = np.array([10, -10, 5, -5, 0])
    if k % 512:
        return np.exp2(np.random.permutation(np.resize(levels, k // 32))).repeat(32)
    a = np.empty((k // 512, 16))
    for p in range(k // 512):
        a[p, :8] = np.random.permutation(np.resize(levels, 8))
        for g in range(8):
            far = levels[np.abs(levels - a[p, g]) >= 10]
            a[p, g + 8] = far[np.random.randint(len(far))]
    return np.exp2(a.ravel()).repeat(32)


def f64(x):
    return np.asarray(x).astype(np.float64)


def striped(idx):
    return np.tile(idx.reshape(-1, 16).T, (8, 1)).astype(np.uint16)


def unstriped(offs):
    return offs[:16].T.reshape(-1).astype(np.int64)


def striped8(idx):
    return np.concatenate([x.reshape(-1, 16).T for x in idx]).astype(np.uint16)


def runs(offs, k):
    lists = np.stack([offs[16 * r : 16 * r + 16].T.reshape(-1) for r in range(8)]).astype(np.int64)
    return lists[np.arange(k) % 512 // 64]


def pack_weight(w):
    k, n = w.shape
    w = f64(np.asarray(w, np.float32).astype(ml_dtypes.bfloat16)).reshape(k // 32, 32, n)
    amax = np.abs(w).max(1)
    byte = np.clip(np.where(amax > 0, np.frexp(amax)[1] - 1 + 127 - 7, 1), 1, 254)
    scaled = (w * np.exp2(127.0 - byte)[:, None, :]).reshape(k, n).astype(np.float32)
    words = np.ascontiguousarray(scaled.reshape(k // 512, 128, 4, n).transpose(0, 1, 3, 2)).astype(ml_dtypes.float8_e4m3fn).view(np.uint8)
    return words, np.ascontiguousarray(byte.astype(np.uint8).reshape(k // 512, 16, n))


def unpack_weight(words, scales):
    g, p, n, _ = words.shape
    vals = np.ascontiguousarray(words).view(ml_dtypes.float8_e4m3fn).astype(np.float64) * np.repeat(np.exp2(scales.astype(np.float64) - 127.0), 8, axis=1)[..., None]
    return vals.transpose(0, 1, 3, 2).reshape(g * 512, n)

def planes(y):
    n, m = y.shape
    v = y.astype(np.float32).astype(ml_dtypes.bfloat16).astype(np.float64).reshape(n // 32, 32, m)
    top = np.abs(v).max(1)
    byte = np.clip(np.where(top > 0, np.frexp(top)[1] - 1 + 127 - 7, 1), 1, 254)
    codes = (v * np.exp2(127.0 - byte)[:, None, :]).reshape(n, m).astype(np.float32).astype(ml_dtypes.float8_e4m3fn).view(np.uint8)
    words = codes.reshape(n // 512, 128, 4, m).transpose(0, 1, 3, 2)
    return np.ascontiguousarray(words), np.ascontiguousarray(byte.astype(np.uint8).reshape(n // 512, 16, m))


K, T, S, N, H = 512, 2048, 512, 512, 512


def setup_inputs():
    n = np.random.standard_normal
    s = mx_kscale(K)[:, None]
    u = mx_kscale(H)
    packed_xT = pack_weight(n((K, T)) * s)
    packed_w1 = pack_weight(n((K, H)) / np.sqrt(K) / s)
    packed_w3 = pack_weight(n((H, N)) / np.sqrt(H) / u[:, None])
    return {
        "x_words": packed_xT[0],
        "x_scales": packed_xT[1],
        "w1_words": packed_w1[0],
        "w1_scales": packed_w1[1],
        "w2": (n((K, H)) / np.sqrt(K) / s * u).astype(np.float32),
        "w3_words": packed_w3[0],
        "w3_scales": packed_w3[1],
        "offs": striped(np.random.permutation(T)[:S]),
        "p1": striped8(np.stack([np.random.permutation(S) for _ in range(8)])),
        "p2": striped8(np.stack([np.random.permutation(S) for _ in range(8)])),
    }


def reference(x_words, x_scales, w1_words, w1_scales, w2, w3_words, w3_scales, offs, p1, p2):
    xq = unpack_weight(x_words, x_scales)[:, unstriped(offs)]
    val = mxq(f64(w2), 0, "e4m3").T @ xq
    c = unpack_weight(w1_words, w1_scales).T @ xq
    e1 = np.exp(-0.5 * ((c - (c[np.arange(H)[:, None], runs(p1, H)])) ** 2))
    e2 = np.exp(-0.5 * ((c - (c[np.arange(H)[:, None], runs(p2, H)])) ** 2))
    z = (val + e1 * (val[np.arange(H)[:, None], runs(p1, H)]) + e2 * (val[np.arange(H)[:, None], runs(p2, H)])) / (e1 + e2 + 1)
    out_0 = unpack_weight(w3_words, w3_scales).T @ mxq(z, 0, "e4m3")
    return (out_0,) + planes(out_0)

@@ -1,0 +1,237 @@
+from contextlib import ExitStack
+
+import concourse.mybir as mybir
+from concourse.masks import make_identity
+
+K, T, S, H, N = 512, 2048, 512, 512, 512
+FLOPS = 2 * S * (K * H + K * H + H * N)
+
+F32 = mybir.dt.float32
+BF16 = mybir.dt.bfloat16
+I32 = mybir.dt.int32
+U32 = mybir.dt.uint32
+U16 = mybir.dt.uint16
+U8 = mybir.dt.uint8
+FP8X4 = mybir.dt.float8_e4m3fn_x4
+ACT = mybir.ActivationFunctionType
+ALU = mybir.AluOpType
+
+P = 128
+PACK = 4
+BLOCK = 128
+BLOCKS = S // BLOCK
+CHUNK = 256
+LIST_COLS = S // 16
+
+
+def load_scale_rows(nc, plane, scales):
+    for q in range(4):
+        nc.sync.dma_start(
+            out=plane[32 * q : 32 * q + 4, :].bitcast(I32),
+            in_=scales[0, 4 * q : 4 * q + 4, :].bitcast(I32),
+        )
+
+
+def load_words(nc, tile, words):
+    nc.sync.dma_start(out=tile[:].bitcast(I32), in_=words[0].rearrange("p c r -> p (c r)").bitcast(I32))
+
+
+def deal_columns(nc, dealt, plain):
+    nc.vector.tensor_copy(
+        out=dealt.rearrange("p (t m) -> p m t", t=PACK),
+        in_=plain.rearrange("p (m t) -> p m t", t=PACK),
+    )
+
+
+def tile_picked_nlmean_none_po_kernel(
+    tc, x_words, x_scales, w1_words, w1_scales, w2, w3_words, w3_scales, offs, p1, p2, out_0, out_1, out_2
+):
+    nc = tc.nc
+    with ExitStack() as ctx:
+        lists = ctx.enter_context(tc.tile_pool(name="lists", bufs=1))
+        keep = ctx.enter_context(tc.tile_pool(name="keep", bufs=1))
+        ring = ctx.enter_context(tc.tile_pool(name="ring", bufs=3))
+        psum = ctx.enter_context(tc.psum_pool(name="psum", bufs=2))
+
+        offs_sb = lists.tile([P, LIST_COLS], U16, name="offs_sb")
+        p1_sb = lists.tile([P, LIST_COLS], U16, name="p1_sb")
+        p2_sb = lists.tile([P, LIST_COLS], U16, name="p2_sb")
+
+        x_plane = keep.tile([P, T], U8, name="x_plane", align_bytes=64)
+        x_all = keep.tile([P, T], U32, name="x_all", align_bytes=64)
+        w1_plane_raw = keep.tile([P, H], U8, name="w1_plane_raw", align_bytes=64)
+        w3_plane_raw = keep.tile([P, N], U8, name="w3_plane_raw", align_bytes=64)
+        w1_raw = keep.tile([P, H], I32, name="w1_raw", align_bytes=64)
+        w3_raw = keep.tile([P, N], I32, name="w3_raw", align_bytes=64)
+        zero = keep.tile([P, 1], F32, name="zero")
+        for plane in (x_plane, w1_plane_raw, w3_plane_raw):
+            nc.vector.memset(plane[:].bitcast(I32), 0)
+        nc.vector.memset(zero[:], 0.0)
+
+        c_win = [keep.tile([P, 2 * S], F32, name=f"c_win{t}") for t in range(PACK)]
+        for t in range(PACK):
+            nc.scalar.activation(out=c_win[t][:, S:], in_=zero[:].to_broadcast([P, S]), func=ACT.Copy)
+
+        ident = keep.tile([P, P], F32, name="ident")
+        make_identity(nc, ident[:])
+
+        nc.sync.dma_start(offs_sb[:], offs)
+        load_scale_rows(nc, x_plane, x_scales)
+        load_words(nc, x_all, x_words)
+        load_words(nc, w1_raw, w1_words)
+        load_scale_rows(nc, w1_plane_raw, w1_scales)
+        nc.sync.dma_start(p1_sb[:], p1)
+        w2_rows = w2.rearrange("(p j) c -> p j c", j=PACK)
+        w2_raw = []
+        for h in range(2):
+            half = keep.tile([P, PACK, H // 2], F32, name=f"w2_raw{h}")
+            nc.sync.dma_start(out=half[:], in_=w2_rows[:, :, h * (H // 2) : (h + 1) * (H // 2)])
+            w2_raw.append(half)
+        nc.sync.dma_start(p2_sb[:], p2)
+        load_words(nc, w3_raw, w3_words)
+        load_scale_rows(nc, w3_plane_raw, w3_scales)
+
+        xs = keep.tile([P, S], U8, name="xs", align_bytes=64)
+        xw = keep.tile([P, S], U32, name="xw", align_bytes=64)
+        nc.vector.tensor_copy(out=xs[:], in_=x_plane[:].indirect(offs_sb[:]))
+        w1_w = keep.tile([P, H], I32, name="w1_w", align_bytes=64)
+        w1_s = keep.tile([P, H], U8, name="w1_s", align_bytes=64)
+        nc.vector.tensor_copy(out=xw[:], in_=x_all[:].indirect(offs_sb[:]))
+        deal_columns(nc, w1_w[:], w1_raw[:])
+        deal_columns(nc, w1_s[:], w1_plane_raw[:])
+
+        def product(weights, plane, t, moving, moving_plane, out):
+            cols = slice(t * P, (t + 1) * P)
+            nc.tensor.matmul_mx(
+                out=out,
+                lhsT=weights[:, cols].bitcast(FP8X4),
+                lhsT_scale=plane[:, cols],
+                rhs=moving.bitcast(FP8X4),
+                rhs_scale=moving_plane,
+                start=True,
+                stop=True,
+            )
+
+        c_here = []
+        for t in range(PACK):
+            bank = psum.tile([P, S], F32, name="prod")
+            product(w1_w, w1_s, t, xw[:], xs[:], bank[:])
+            here = keep.tile([P, S], F32, name=f"c_here{t}")
+            nc.scalar.activation(out=c_win[t][:, :S], in_=bank[:], func=ACT.Copy)
+            nc.scalar.activation(out=here[:], in_=bank[:], func=ACT.Copy)
+            c_here.append(here)
+
+        w2_grouped = keep.tile([P, PACK * H], BF16, name="w2_grouped", align_bytes=64)
+        w2_view = w2_grouped[:].rearrange("p (t m j) -> p m t j", t=PACK, j=PACK)
+        for h in range(2):
+            nc.vector.tensor_copy(
+                out=w2_view[:, h * (P // 2) : (h + 1) * (P // 2), :, :],
+                in_=w2_raw[h][:].rearrange("p j (m t) -> p m t j", t=PACK),
+            )
+        w2_w = keep.tile([P, H], U32, name="w2_w", align_bytes=64)
+        w2_s = keep.tile([P, H], U8, name="w2_s", align_bytes=64)
+        nc.vector.quantize_mx(out=w2_w[:].bitcast(FP8X4), scales=w2_s[:], in_=w2_grouped[:])
+
+        def add_transposed(out, terms):
+            for i, term in enumerate(terms):
+                nc.tensor.matmul(
+                    out, lhsT=term, rhs=ident[:], is_transpose=True, start=(i == 0), stop=(i == len(terms) - 1)
+                )
+
+        den_sq = keep.tile([P, PACK, S], F32, name="den_sq")
+        weights = []
+        val = []
+        for t in range(PACK):
+            pair = []
+            for n, order in enumerate((p1_sb, p2_sb)):
+                d = ring.tile([P, S], F32, name="d")
+                nc.vector.tensor_tensor(d[:], c_win[t][:].indirect(order[:]), c_here[t][:], ALU.subtract)
+                q = ring.tile([P, S], F32, name="q")
+                nc.scalar.activation(out=q[:], in_=d[:], func=ACT.Square)
+                e = keep.tile([P, S], F32, name=f"e{t}{n}")
+                nc.scalar.activation(out=e[:], in_=q[:], func=ACT.Exp, scale=-0.5)
+                pair.append(e)
+            weights.append(pair)
+            bank = psum.tile([P, S], F32, name="prod")
+            product(w2_w, w2_s, t, xw[:], xs[:], bank[:])
+            v = keep.tile([P, S], F32, name=f"val{t}")
+            nc.scalar.activation(out=v[:], in_=bank[:], func=ACT.Copy)
+            val.append(v)
+            den = psum.tile([P, S], F32, name="den")
+            for b in range(BLOCKS):
+                cols = slice(b * BLOCK, (b + 1) * BLOCK)
+                add_transposed(den[:, cols], [pair[0][:, cols], pair[1][:, cols]])
+            nc.scalar.activation(out=den_sq[:, t, :], in_=den[:], func=ACT.Square, bias=1.0)
+
+        w3_w = keep.tile([P, N], I32, name="w3_w", align_bytes=64)
+        w3_s = keep.tile([P, N], U8, name="w3_s", align_bytes=64)
+        deal_columns(nc, w3_w[:], w3_raw[:])
+        deal_columns(nc, w3_s[:], w3_plane_raw[:])
+
+        y_words = keep.tile([P, S], U32, name="y_words", align_bytes=64)
+        y_plane = keep.tile([P, S], U8, name="y_plane", align_bytes=64)
+        out_rows = out_0.rearrange("(p t) j -> p t j", t=PACK)
+        out_words = out_1[0].rearrange("p c r -> p (c r)").bitcast(I32)
+
+        per_chunk = CHUNK // BLOCK
+        for h in range(S // CHUNK):
+            chunk = slice(h * CHUNK, (h + 1) * CHUNK)
+            list_cols = slice(h * CHUNK // 16, (h + 1) * CHUNK // 16)
+            nums = [psum.tile([P, PACK * P], F32, name="num", bufs=4) for b in range(per_chunk)]
+            for t in range(PACK):
+                terms = []
+                for n, order in enumerate((p1_sb, p2_sb)):
+                    term = ring.tile([P, CHUNK], F32, name=f"term{n}")
+                    nc.vector.tensor_tensor(
+                        term[:], val[t][:].indirect(order[:, list_cols]), weights[t][n][:, chunk], ALU.mult
+                    )
+                    terms.append(term)
+                for i in range(per_chunk):
+                    b = h * per_chunk + i
+                    local = slice(i * BLOCK, (i + 1) * BLOCK)
+                    add_transposed(
+                        nums[i][:, t * P : (t + 1) * P],
+                        [val[t][:, b * BLOCK : (b + 1) * BLOCK], terms[0][:, local], terms[1][:, local]],
+                    )
+            for i in range(per_chunk):
+                b = h * per_chunk + i
+                cols = slice(b * BLOCK, (b + 1) * BLOCK)
+                inv = ring.tile([P, 2, P, 2], F32, name="inv")
+                nc.scalar.activation(
+                    out=inv[:],
+                    in_=den_sq[:, :, cols].rearrange("j (u e) p -> j u p e", e=2),
+                    func=ACT.Abs_reciprocal_sqrt,
+                )
+                z_t = ring.tile([P, 2, P, 2], BF16, name="z_t", align_bytes=64)
+                nc.vector.tensor_tensor(
+                    z_t[:], nums[i][:].rearrange("j (u e p) -> j u p e", u=2, e=2), inv[:], ALU.mult
+                )
+                z_words = z_t[:].rearrange("j u p e -> j (u p e)").bitcast(F32)
+                back = psum.tile([P, 2, BLOCK], F32, name="den")
+                for u in range(2):
+                    nc.tensor.transpose(back[:, u, :], z_words[:, u * P : (u + 1) * P], ident[:])
+                z = ring.tile([P, PACK * BLOCK], BF16, name="z", align_bytes=64)
+                nc.scalar.copy(
+                    out=z[:].bitcast(F32).rearrange("p (j u) -> p j u", u=2), in_=back[:].rearrange("p u j -> p j u")
+                )
+                z_w = ring.tile([P, BLOCK], U32, name="z_w", align_bytes=64)
+                z_s = ring.tile([P, BLOCK], U8, name="z_s", align_bytes=64)
+                nc.vector.quantize_mx(out=z_w[:].bitcast(FP8X4), scales=z_s[:], in_=z[:])
+                y_bank = psum.tile([P, PACK, BLOCK], F32, name="prod")
+                for t in range(PACK):
+                    product(w3_w, w3_s, t, z_w[:], z_s[:], y_bank[:, t, :])
+                y = ring.tile([P, PACK, BLOCK], F32, name="y")
+                nc.scalar.activation(out=y[:], in_=y_bank[:], func=ACT.Copy)
+                nc.sync.dma_start(out=out_rows[:, :, cols], in_=y[:])
+                y_grouped = ring.tile([P, BLOCK, PACK], BF16, name="y_grouped", align_bytes=64)
+                nc.vector.tensor_copy(out=y_grouped[:], in_=y[:].rearrange("p t j -> p j t"))
+                nc.vector.quantize_mx(
+                    out=y_words[:, cols].bitcast(FP8X4),
+                    scales=y_plane[:, cols],
+                    in_=y_grouped[:].rearrange("p j t -> p (j t)"),
+                )
+            nc.sync.dma_start(out=out_words[:, chunk], in_=y_words[:, chunk].bitcast(I32))
+        for q in range(4):
+            nc.sync.dma_start(
+                out=out_2[0, 4 * q : 4 * q + 4, :].bitcast(I32), in_=y_plane[32 * q : 32 * q + 4, :].bitcast(I32)
+            )

@@ -20,7 +20,7 @@ P = 128
 PACK = 4
 BLOCK = 128
 BLOCKS = S // BLOCK
-CHUNK = 256
+FIRST_BY_DMA = 1
 LIST_COLS = S // 16
 
 
@@ -36,10 +36,10 @@ def load_words(nc, tile, words):
     nc.sync.dma_start(out=tile[:].bitcast(I32), in_=words[0].rearrange("p c r -> p (c r)").bitcast(I32))
 
 
-def deal_columns(nc, dealt, plain):
+def deal_columns(nc, dealt, plain, first=0, last=PACK):
     nc.vector.tensor_copy(
-        out=dealt.rearrange("p (t m) -> p m t", t=PACK),
-        in_=plain.rearrange("p (m t) -> p m t", t=PACK),
+        out=dealt.rearrange("p (t m) -> p m t", t=PACK)[:, :, first:last],
+        in_=plain.rearrange("p (m t) -> p m t", t=PACK)[:, :, first:last],
     )
 
 
@@ -68,7 +68,7 @@ def tile_picked_nlmean_none_po_kernel(
             nc.vector.memset(plane[:].bitcast(I32), 0)
         nc.vector.memset(zero[:], 0.0)
 
-        c_win = [keep.tile([P, 2 * S], F32, name=f"c_win{t}") for t in range(PACK)]
+        c_win = [keep.tile([P, 2 * S], F32, name=f"c_win{t}", tag=f"c_win{t}") for t in range(PACK)]
         for t in range(PACK):
             nc.scalar.activation(out=c_win[t][:, S:], in_=zero[:].to_broadcast([P, S]), func=ACT.Copy)
 
@@ -76,29 +76,30 @@ def tile_picked_nlmean_none_po_kernel(
         make_identity(nc, ident[:])
 
         nc.sync.dma_start(offs_sb[:], offs)
+        nc.sync.dma_start(p1_sb[:], p1)
+        nc.sync.dma_start(p2_sb[:], p2)
         load_scale_rows(nc, x_plane, x_scales)
         load_words(nc, x_all, x_words)
         load_words(nc, w1_raw, w1_words)
         load_scale_rows(nc, w1_plane_raw, w1_scales)
-        nc.sync.dma_start(p1_sb[:], p1)
         w2_rows = w2.rearrange("(p j) c -> p j c", j=PACK)
         w2_raw = []
         for h in range(2):
             half = keep.tile([P, PACK, H // 2], F32, name=f"w2_raw{h}")
             nc.sync.dma_start(out=half[:], in_=w2_rows[:, :, h * (H // 2) : (h + 1) * (H // 2)])
             w2_raw.append(half)
-        nc.sync.dma_start(p2_sb[:], p2)
         load_words(nc, w3_raw, w3_words)
         load_scale_rows(nc, w3_plane_raw, w3_scales)
 
         xs = keep.tile([P, S], U8, name="xs", align_bytes=64)
         xw = keep.tile([P, S], U32, name="xw", align_bytes=64)
-        nc.vector.tensor_copy(out=xs[:], in_=x_plane[:].indirect(offs_sb[:]))
         w1_w = keep.tile([P, H], I32, name="w1_w", align_bytes=64)
         w1_s = keep.tile([P, H], U8, name="w1_s", align_bytes=64)
+        nc.vector.tensor_copy(out=xs[:], in_=x_plane[:].indirect(offs_sb[:]))
         nc.vector.tensor_copy(out=xw[:], in_=x_all[:].indirect(offs_sb[:]))
         deal_columns(nc, w1_w[:], w1_raw[:])
-        deal_columns(nc, w1_s[:], w1_plane_raw[:])
+        deal_columns(nc, w1_s[:], w1_plane_raw[:], 0, 1)
+        deal_columns(nc, w1_s[:], w1_plane_raw[:], 1, PACK)
 
         def product(weights, plane, t, moving, moving_plane, out):
             cols = slice(t * P, (t + 1) * P)
@@ -112,126 +113,183 @@ def tile_picked_nlmean_none_po_kernel(
                 stop=True,
             )
 
-        c_here = []
-        for t in range(PACK):
-            bank = psum.tile([P, S], F32, name="prod")
-            product(w1_w, w1_s, t, xw[:], xs[:], bank[:])
-            here = keep.tile([P, S], F32, name=f"c_here{t}")
-            nc.scalar.activation(out=c_win[t][:, :S], in_=bank[:], func=ACT.Copy)
-            nc.scalar.activation(out=here[:], in_=bank[:], func=ACT.Copy)
-            c_here.append(here)
-
         w2_grouped = keep.tile([P, PACK * H], BF16, name="w2_grouped", align_bytes=64)
         w2_view = w2_grouped[:].rearrange("p (t m j) -> p m t j", t=PACK, j=PACK)
-        for h in range(2):
-            nc.vector.tensor_copy(
-                out=w2_view[:, h * (P // 2) : (h + 1) * (P // 2), :, :],
-                in_=w2_raw[h][:].rearrange("p j (m t) -> p m t j", t=PACK),
-            )
+        nc.scalar.activation(
+            out=w2_view[:, : P // 2, :, :], in_=w2_raw[0][:].rearrange("p j (m t) -> p m t j", t=PACK), func=ACT.Copy
+        )
+
+        val_win = [keep.tile([P, 2 * S], F32, name=f"val_win{t}") for t in range(PACK)]
+        for t in range(PACK):
+            bank = psum.tile([P, S], F32, name="prod", bufs=4)
+            product(w1_w, w1_s, t, xw[:], xs[:], bank[:])
+            nc.scalar.activation(out=c_win[t][:, :S], in_=bank[:], func=ACT.Copy)
+            if t < FIRST_BY_DMA:
+                nc.scalar.activation(out=val_win[t][:, S:], in_=bank[:], func=ACT.Copy)
+            else:
+                nc.sync.dma_start(out=val_win[t][:, S:], in_=c_win[t][:, :S])
+
+        diffs = []
+
+        def differences(t):
+            for order in (p1_sb, p2_sb):
+                d = ring.tile([P, S], F32, name="d", bufs=2 * PACK)
+                nc.vector.tensor_tensor(d[:], c_win[t][:].indirect(order[:]), val_win[t][:, S:], ALU.subtract)
+                diffs.append(d)
+
+        differences(0)
+        nc.vector.tensor_copy(out=w2_view[:, P // 2 :, :, :], in_=w2_raw[1][:].rearrange("p j (m t) -> p m t j", t=PACK))
         w2_w = keep.tile([P, H], U32, name="w2_w", align_bytes=64)
         w2_s = keep.tile([P, H], U8, name="w2_s", align_bytes=64)
         nc.vector.quantize_mx(out=w2_w[:].bitcast(FP8X4), scales=w2_s[:], in_=w2_grouped[:])
 
-        def add_transposed(out, terms):
-            for i, term in enumerate(terms):
-                nc.tensor.matmul(
-                    out, lhsT=term, rhs=ident[:], is_transpose=True, start=(i == 0), stop=(i == len(terms) - 1)
-                )
+        for t in range(1, PACK):
+            differences(t)
 
-        den_sq = keep.tile([P, PACK, S], F32, name="den_sq")
-        weights = []
-        val = []
-        for t in range(PACK):
-            pair = []
-            for n, order in enumerate((p1_sb, p2_sb)):
-                d = ring.tile([P, S], F32, name="d")
-                nc.vector.tensor_tensor(d[:], c_win[t][:].indirect(order[:]), c_here[t][:], ALU.subtract)
-                q = ring.tile([P, S], F32, name="q")
-                nc.scalar.activation(out=q[:], in_=d[:], func=ACT.Square)
-                e = keep.tile([P, S], F32, name=f"e{t}{n}")
-                nc.scalar.activation(out=e[:], in_=q[:], func=ACT.Exp, scale=-0.5)
-                pair.append(e)
-            weights.append(pair)
-            bank = psum.tile([P, S], F32, name="prod")
+        def values(t):
+            bank = psum.tile([P, S], F32, name="prod", bufs=4)
             product(w2_w, w2_s, t, xw[:], xs[:], bank[:])
-            v = keep.tile([P, S], F32, name=f"val{t}")
-            nc.scalar.activation(out=v[:], in_=bank[:], func=ACT.Copy)
-            val.append(v)
-            den = psum.tile([P, S], F32, name="den")
-            for b in range(BLOCKS):
-                cols = slice(b * BLOCK, (b + 1) * BLOCK)
-                add_transposed(den[:, cols], [pair[0][:, cols], pair[1][:, cols]])
-            nc.scalar.activation(out=den_sq[:, t, :], in_=den[:], func=ACT.Square, bias=1.0)
+            nc.scalar.activation(out=val_win[t][:, :S], in_=bank[:], func=ACT.Copy)
 
-        w3_w = keep.tile([P, N], I32, name="w3_w", align_bytes=64)
-        w3_s = keep.tile([P, N], U8, name="w3_s", align_bytes=64)
-        deal_columns(nc, w3_w[:], w3_raw[:])
-        deal_columns(nc, w3_s[:], w3_plane_raw[:])
+        dens = [psum.tile([P, PACK * P], F32, name=f"den{b}", tag=f"sum{b}", bufs=1) for b in range(BLOCKS)]
+        weights = {}
+        for t in range(PACK):
+            pieces = 1
+            width = S // pieces
+            for n in range(2):
+                q = ring.tile([P, S], F32, name="q")
+                nc.scalar.activation(out=q[:], in_=diffs[2 * t + n][:], func=ACT.Square)
+                for h in range(pieces):
+                    e = keep.tile([P, width], F32, name=f"e{t}{n}{h}", tag=f"e{t}{n}{h}", align_bytes=64)
+                    nc.scalar.activation(out=e[:], in_=q[:, h * width : (h + 1) * width], func=ACT.Exp, scale=-0.5)
+                    weights[t, n, h] = e
+                    for i in range(width // BLOCK):
+                        nc.tensor.matmul(
+                            dens[h * 2 + i][:, t * P : (t + 1) * P],
+                            lhsT=e[:, i * BLOCK : (i + 1) * BLOCK],
+                            rhs=ident[:],
+                            is_transpose=True,
+                            start=(n == 0),
+                            stop=(n == 1),
+                        )
+            if t == 1:
+                values(0)
+        values(1)
+
+        den_sq = []
+        for b in range(BLOCKS):
+            sq = ring.tile([P, PACK * P], F32, name="den_sq", bufs=4)
+            nc.scalar.activation(out=sq[:], in_=dens[b][:], func=ACT.Square, bias=1.0)
+            den_sq.append(sq)
+        values(2)
+        values(3)
 
         y_words = keep.tile([P, S], U32, name="y_words", align_bytes=64)
         y_plane = keep.tile([P, S], U8, name="y_plane", align_bytes=64)
         out_rows = out_0.rearrange("(p t) j -> p t j", t=PACK)
         out_words = out_1[0].rearrange("p c r -> p (c r)").bitcast(I32)
 
-        per_chunk = CHUNK // BLOCK
-        for h in range(S // CHUNK):
-            chunk = slice(h * CHUNK, (h + 1) * CHUNK)
-            list_cols = slice(h * CHUNK // 16, (h + 1) * CHUNK // 16)
-            nums = [psum.tile([P, PACK * P], F32, name="num", bufs=4) for b in range(per_chunk)]
-            for t in range(PACK):
-                terms = []
-                for n, order in enumerate((p1_sb, p2_sb)):
-                    term = ring.tile([P, CHUNK], F32, name=f"term{n}")
-                    nc.vector.tensor_tensor(
-                        term[:], val[t][:].indirect(order[:, list_cols]), weights[t][n][:, chunk], ALU.mult
-                    )
-                    terms.append(term)
-                for i in range(per_chunk):
-                    b = h * per_chunk + i
-                    local = slice(i * BLOCK, (i + 1) * BLOCK)
-                    add_transposed(
-                        nums[i][:, t * P : (t + 1) * P],
-                        [val[t][:, b * BLOCK : (b + 1) * BLOCK], terms[0][:, local], terms[1][:, local]],
-                    )
-            for i in range(per_chunk):
-                b = h * per_chunk + i
-                cols = slice(b * BLOCK, (b + 1) * BLOCK)
-                inv = ring.tile([P, 2, P, 2], F32, name="inv")
-                nc.scalar.activation(
-                    out=inv[:],
-                    in_=den_sq[:, :, cols].rearrange("j (u e) p -> j u p e", e=2),
-                    func=ACT.Abs_reciprocal_sqrt,
-                )
-                z_t = ring.tile([P, 2, P, 2], BF16, name="z_t", align_bytes=64)
+        nums = [psum.tile([P, PACK * P], F32, name=f"num{b}", tag=f"sum{b}", bufs=1) for b in range(BLOCKS)]
+
+        def weighted_neighbours(t, h, count, tag):
+            first = h * count
+            list_cols = slice(first * BLOCK // 16, (first + count) * BLOCK // 16)
+            both = keep.tile([P, 2, count * BLOCK], F32, name=f"terms{t}{h}", tag=tag)
+            for n, order in enumerate((p1_sb, p2_sb)):
                 nc.vector.tensor_tensor(
-                    z_t[:], nums[i][:].rearrange("j (u e p) -> j u p e", u=2, e=2), inv[:], ALU.mult
+                    both[:, n, :], val_win[t][:].indirect(order[:, list_cols]), weights[t, n, 0][:, first * BLOCK : (first + count) * BLOCK], ALU.mult
                 )
-                z_words = z_t[:].rearrange("j u p e -> j (u p e)").bitcast(F32)
-                back = psum.tile([P, 2, BLOCK], F32, name="den")
-                for u in range(2):
-                    nc.tensor.transpose(back[:, u, :], z_words[:, u * P : (u + 1) * P], ident[:])
-                z = ring.tile([P, PACK * BLOCK], BF16, name="z", align_bytes=64)
-                nc.scalar.copy(
-                    out=z[:].bitcast(F32).rearrange("p (j u) -> p j u", u=2), in_=back[:].rearrange("p u j -> p j u")
-                )
-                z_w = ring.tile([P, BLOCK], U32, name="z_w", align_bytes=64)
-                z_s = ring.tile([P, BLOCK], U8, name="z_s", align_bytes=64)
-                nc.vector.quantize_mx(out=z_w[:].bitcast(FP8X4), scales=z_s[:], in_=z[:])
-                y_bank = psum.tile([P, PACK, BLOCK], F32, name="prod")
+            sources = (val_win[t][:, first * BLOCK : (first + count) * BLOCK], both[:, 0, :], both[:, 1, :])
+            for k, source in enumerate(sources):
+                for i in range(count):
+                    nc.tensor.matmul(
+                        nums[first + i][:, t * P : (t + 1) * P],
+                        lhsT=source[:, i * BLOCK : (i + 1) * BLOCK],
+                        rhs=ident[:],
+                        is_transpose=True,
+                        start=(k == 0),
+                        stop=(k == len(sources) - 1),
+                    )
+
+        invs = []
+        for b in range(BLOCKS):
+            inv = keep.tile([P, 2, P, 2], F32, name=f"inv{b}", tag=f"inv{b}")
+            nc.scalar.activation(
+                out=inv[:],
+                in_=den_sq[b][:].rearrange("j (u e p) -> j u p e", u=2, e=2),
+                func=ACT.Abs_reciprocal_sqrt,
+            )
+            invs.append(inv)
+
+        z_ts = []
+
+        def normalise(b):
+            z_t = ring.tile([P, 2, P, 2], BF16, name="z_t", align_bytes=64, bufs=4)
+            nc.vector.tensor_tensor(
+                z_t[:], nums[b][:].rearrange("j (u e p) -> j u p e", u=2, e=2), invs[b][:], ALU.mult
+            )
+            z_ts.append(z_t)
+
+        w3_w = keep.tile([P, N], I32, name="w3_w", align_bytes=64)
+        w3_s = keep.tile([P, N], U8, name="w3_s", align_bytes=64)
+        deal_columns(nc, w3_s[:], w3_plane_raw[:])
+        deal_columns(nc, w3_w[:], w3_raw[:])
+        for t in range(PACK - 1):
+            weighted_neighbours(t, 0, BLOCKS, f"c_win{PACK - 1 - t}")
+        weighted_neighbours(PACK - 1, 0, 2, "c_win0")
+        weighted_neighbours(PACK - 1, 1, 2, "last_terms")
+        for b in range(BLOCKS):
+            normalise(b)
+
+        z_mx = []
+        for b in range(BLOCKS):
+            z_words = z_ts[b][:].rearrange("j u p e -> j (u p e)").bitcast(F32)
+            back = psum.tile([P, 2, BLOCK], F32, name="prod", bufs=4)
+            for u in range(2):
+                nc.tensor.transpose(back[:, u, :], z_words[:, u * P : (u + 1) * P], ident[:])
+            z = ring.tile([P, PACK * BLOCK], BF16, name="z", align_bytes=64, bufs=4)
+            nc.scalar.copy(
+                out=z[:].bitcast(F32).rearrange("p (j u) -> p j u", u=2), in_=back[:].rearrange("p u j -> p j u")
+            )
+            z_w = ring.tile([P, BLOCK], U32, name="z_w", align_bytes=64, bufs=4)
+            z_s = ring.tile([P, BLOCK], U8, name="z_s", align_bytes=64, bufs=4)
+            nc.vector.quantize_mx(out=z_w[:].bitcast(FP8X4), scales=z_s[:], in_=z[:])
+            z_mx.append((z_w, z_s))
+
+        ys = []
+        for b in range(BLOCKS):
+            cols = slice(b * BLOCK, (b + 1) * BLOCK)
+            z_w, z_s = z_mx[b]
+            y = ring.tile([P, PACK, BLOCK], F32, name="y", bufs=4)
+            if b < BLOCKS - 1:
+                y_bank = psum.tile([P, PACK, BLOCK], F32, name=f"y_bank{b}", tag=f"sum{b}", bufs=1)
                 for t in range(PACK):
                     product(w3_w, w3_s, t, z_w[:], z_s[:], y_bank[:, t, :])
-                y = ring.tile([P, PACK, BLOCK], F32, name="y")
                 nc.scalar.activation(out=y[:], in_=y_bank[:], func=ACT.Copy)
-                nc.sync.dma_start(out=out_rows[:, :, cols], in_=y[:])
-                y_grouped = ring.tile([P, BLOCK, PACK], BF16, name="y_grouped", align_bytes=64)
-                nc.vector.tensor_copy(out=y_grouped[:], in_=y[:].rearrange("p t j -> p j t"))
-                nc.vector.quantize_mx(
-                    out=y_words[:, cols].bitcast(FP8X4),
-                    scales=y_plane[:, cols],
-                    in_=y_grouped[:].rearrange("p j t -> p (j t)"),
-                )
-            nc.sync.dma_start(out=out_words[:, chunk], in_=y_words[:, chunk].bitcast(I32))
+            else:
+                low = psum.tile([P, 2, BLOCK], F32, name="y_low", tag=f"sum{b}", bufs=1)
+                high = psum.tile([P, 2, BLOCK], F32, name="prod", bufs=4)
+                for t in range(PACK):
+                    product(w3_w, w3_s, t, z_w[:], z_s[:], (low, high)[t // 2][:, t % 2, :])
+                nc.vector.tensor_copy(out=y[:, 0:2, :], in_=low[:])
+                nc.scalar.activation(out=y[:, 2:4, :], in_=high[:], func=ACT.Copy)
+            nc.sync.dma_start(out=out_rows[:, :, cols], in_=y[:])
+            ys.append(y)
+
+        for b in range(BLOCKS):
+            cols = slice(b * BLOCK, (b + 1) * BLOCK)
+            y_grouped = ring.tile([P, BLOCK, PACK], BF16, name="y_grouped", align_bytes=64, bufs=4)
+            nc.vector.tensor_copy(out=y_grouped[:], in_=ys[b][:].rearrange("p t j -> p j t"))
+            nc.vector.quantize_mx(
+                out=y_words[:, cols].bitcast(FP8X4),
+                scales=y_plane[:, cols],
+                in_=y_grouped[:].rearrange("p j t -> p (j t)"),
+            )
+            if b >= BLOCKS - 2:
+                done = slice(0, (b + 1) * BLOCK) if b == BLOCKS - 2 else cols
+                nc.scalar.dma_start(out=out_words[:, done], in_=y_words[:, done].bitcast(I32))
         for q in range(4):
-            nc.sync.dma_start(
+            queue = nc.sync if q % 2 == 0 else nc.scalar
+            queue.dma_start(
                 out=out_2[0, 4 * q : 4 * q + 4, :].bitcast(I32), in_=y_plane[32 * q : 32 * q + 4, :].bitcast(I32)
             )

from contextlib import ExitStack

import concourse.mybir as mybir
from concourse.masks import make_identity

K, T, S, H, N = 512, 2048, 512, 512, 512
FLOPS = 2 * S * (K * H + K * H + H * N)

F32 = mybir.dt.float32
BF16 = mybir.dt.bfloat16
I32 = mybir.dt.int32
U32 = mybir.dt.uint32
U16 = mybir.dt.uint16
U8 = mybir.dt.uint8
FP8X4 = mybir.dt.float8_e4m3fn_x4
ACT = mybir.ActivationFunctionType
ALU = mybir.AluOpType

P = 128
PACK = 4
BLOCK = 128
BLOCKS = S // BLOCK
FIRST_BY_DMA = 1
LIST_COLS = S // 16


def load_scale_rows(nc, plane, scales):
    for q in range(4):
        nc.sync.dma_start(
            out=plane[32 * q : 32 * q + 4, :].bitcast(I32),
            in_=scales[0, 4 * q : 4 * q + 4, :].bitcast(I32),
        )


def load_words(nc, tile, words):
    nc.sync.dma_start(out=tile[:].bitcast(I32), in_=words[0].rearrange("p c r -> p (c r)").bitcast(I32))


def deal_columns(nc, dealt, plain, first=0, last=PACK):
    nc.vector.tensor_copy(
        out=dealt.rearrange("p (t m) -> p m t", t=PACK)[:, :, first:last],
        in_=plain.rearrange("p (m t) -> p m t", t=PACK)[:, :, first:last],
    )


def tile_picked_nlmean_none_po_kernel(
    tc, x_words, x_scales, w1_words, w1_scales, w2, w3_words, w3_scales, offs, p1, p2, out_0, out_1, out_2
):
    nc = tc.nc
    with ExitStack() as ctx:
        lists = ctx.enter_context(tc.tile_pool(name="lists", bufs=1))
        keep = ctx.enter_context(tc.tile_pool(name="keep", bufs=1))
        ring = ctx.enter_context(tc.tile_pool(name="ring", bufs=3))
        psum = ctx.enter_context(tc.psum_pool(name="psum", bufs=2))

        offs_sb = lists.tile([P, LIST_COLS], U16, name="offs_sb")
        p1_sb = lists.tile([P, LIST_COLS], U16, name="p1_sb")
        p2_sb = lists.tile([P, LIST_COLS], U16, name="p2_sb")

        x_plane = keep.tile([P, T], U8, name="x_plane", align_bytes=64)
        x_all = keep.tile([P, T], U32, name="x_all", align_bytes=64)
        w1_plane_raw = keep.tile([P, H], U8, name="w1_plane_raw", align_bytes=64)
        w3_plane_raw = keep.tile([P, N], U8, name="w3_plane_raw", align_bytes=64)
        w1_raw = keep.tile([P, H], I32, name="w1_raw", align_bytes=64)
        w3_raw = keep.tile([P, N], I32, name="w3_raw", align_bytes=64)
        zero = keep.tile([P, 1], F32, name="zero")
        for plane in (x_plane, w1_plane_raw, w3_plane_raw):
            nc.vector.memset(plane[:].bitcast(I32), 0)
        nc.vector.memset(zero[:], 0.0)

        c_win = [keep.tile([P, 2 * S], F32, name=f"c_win{t}", tag=f"c_win{t}") for t in range(PACK)]
        for t in range(PACK):
            nc.scalar.activation(out=c_win[t][:, S:], in_=zero[:].to_broadcast([P, S]), func=ACT.Copy)

        ident = keep.tile([P, P], F32, name="ident")
        make_identity(nc, ident[:])

        nc.sync.dma_start(offs_sb[:], offs)
        nc.sync.dma_start(p1_sb[:], p1)
        nc.sync.dma_start(p2_sb[:], p2)
        load_scale_rows(nc, x_plane, x_scales)
        load_words(nc, x_all, x_words)
        load_words(nc, w1_raw, w1_words)
        load_scale_rows(nc, w1_plane_raw, w1_scales)
        w2_rows = w2.rearrange("(p j) c -> p j c", j=PACK)
        w2_raw = []
        for h in range(2):
            half = keep.tile([P, PACK, H // 2], F32, name=f"w2_raw{h}")
            nc.sync.dma_start(out=half[:], in_=w2_rows[:, :, h * (H // 2) : (h + 1) * (H // 2)])
            w2_raw.append(half)
        load_words(nc, w3_raw, w3_words)
        load_scale_rows(nc, w3_plane_raw, w3_scales)

        xs = keep.tile([P, S], U8, name="xs", align_bytes=64)
        xw = keep.tile([P, S], U32, name="xw", align_bytes=64)
        w1_w = keep.tile([P, H], I32, name="w1_w", align_bytes=64)
        w1_s = keep.tile([P, H], U8, name="w1_s", align_bytes=64)
        nc.vector.tensor_copy(out=xs[:], in_=x_plane[:].indirect(offs_sb[:]))
        nc.vector.tensor_copy(out=xw[:], in_=x_all[:].indirect(offs_sb[:]))
        deal_columns(nc, w1_w[:], w1_raw[:])
        deal_columns(nc, w1_s[:], w1_plane_raw[:], 0, 1)
        deal_columns(nc, w1_s[:], w1_plane_raw[:], 1, PACK)

        def product(weights, plane, t, moving, moving_plane, out):
            cols = slice(t * P, (t + 1) * P)
            nc.tensor.matmul_mx(
                out=out,
                lhsT=weights[:, cols].bitcast(FP8X4),
                lhsT_scale=plane[:, cols],
                rhs=moving.bitcast(FP8X4),
                rhs_scale=moving_plane,
                start=True,
                stop=True,
            )

        w2_grouped = keep.tile([P, PACK * H], BF16, name="w2_grouped", align_bytes=64)
        w2_view = w2_grouped[:].rearrange("p (t m j) -> p m t j", t=PACK, j=PACK)
        nc.scalar.activation(
            out=w2_view[:, : P // 2, :, :], in_=w2_raw[0][:].rearrange("p j (m t) -> p m t j", t=PACK), func=ACT.Copy
        )

        val_win = [keep.tile([P, 2 * S], F32, name=f"val_win{t}") for t in range(PACK)]
        for t in range(PACK):
            bank = psum.tile([P, S], F32, name="prod", bufs=4)
            product(w1_w, w1_s, t, xw[:], xs[:], bank[:])
            nc.scalar.activation(out=c_win[t][:, :S], in_=bank[:], func=ACT.Copy)
            if t < FIRST_BY_DMA:
                nc.scalar.activation(out=val_win[t][:, S:], in_=bank[:], func=ACT.Copy)
            else:
                nc.sync.dma_start(out=val_win[t][:, S:], in_=c_win[t][:, :S])

        diffs = []

        def differences(t):
            for order in (p1_sb, p2_sb):
                d = ring.tile([P, S], F32, name="d", bufs=2 * PACK)
                nc.vector.tensor_tensor(d[:], c_win[t][:].indirect(order[:]), val_win[t][:, S:], ALU.subtract)
                diffs.append(d)

        differences(0)
        nc.vector.tensor_copy(out=w2_view[:, P // 2 :, :, :], in_=w2_raw[1][:].rearrange("p j (m t) -> p m t j", t=PACK))
        w2_w = keep.tile([P, H], U32, name="w2_w", align_bytes=64)
        w2_s = keep.tile([P, H], U8, name="w2_s", align_bytes=64)
        nc.vector.quantize_mx(out=w2_w[:].bitcast(FP8X4), scales=w2_s[:], in_=w2_grouped[:])

        for t in range(1, PACK):
            differences(t)

        def values(t):
            bank = psum.tile([P, S], F32, name="prod", bufs=4)
            product(w2_w, w2_s, t, xw[:], xs[:], bank[:])
            nc.scalar.activation(out=val_win[t][:, :S], in_=bank[:], func=ACT.Copy)

        dens = [psum.tile([P, PACK * P], F32, name=f"den{b}", tag=f"sum{b}", bufs=1) for b in range(BLOCKS)]
        weights = {}
        for t in range(PACK):
            pieces = 1
            width = S // pieces
            for n in range(2):
                q = ring.tile([P, S], F32, name="q")
                nc.scalar.activation(out=q[:], in_=diffs[2 * t + n][:], func=ACT.Square)
                for h in range(pieces):
                    e = keep.tile([P, width], F32, name=f"e{t}{n}{h}", tag=f"e{t}{n}{h}", align_bytes=64)
                    nc.scalar.activation(out=e[:], in_=q[:, h * width : (h + 1) * width], func=ACT.Exp, scale=-0.5)
                    weights[t, n, h] = e
                    for i in range(width // BLOCK):
                        nc.tensor.matmul(
                            dens[h * 2 + i][:, t * P : (t + 1) * P],
                            lhsT=e[:, i * BLOCK : (i + 1) * BLOCK],
                            rhs=ident[:],
                            is_transpose=True,
                            start=(n == 0),
                            stop=(n == 1),
                        )
            if t == 1:
                values(0)
        values(1)

        den_sq = []
        for b in range(BLOCKS):
            sq = ring.tile([P, PACK * P], F32, name="den_sq", bufs=4)
            nc.scalar.activation(out=sq[:], in_=dens[b][:], func=ACT.Square, bias=1.0)
            den_sq.append(sq)
        values(2)
        values(3)

        y_words = keep.tile([P, S], U32, name="y_words", align_bytes=64)
        y_plane = keep.tile([P, S], U8, name="y_plane", align_bytes=64)
        out_rows = out_0.rearrange("(p t) j -> p t j", t=PACK)
        out_words = out_1[0].rearrange("p c r -> p (c r)").bitcast(I32)

        nums = [psum.tile([P, PACK * P], F32, name=f"num{b}", tag=f"sum{b}", bufs=1) for b in range(BLOCKS)]

        def weighted_neighbours(t, h, count, tag):
            first = h * count
            list_cols = slice(first * BLOCK // 16, (first + count) * BLOCK // 16)
            both = keep.tile([P, 2, count * BLOCK], F32, name=f"terms{t}{h}", tag=tag)
            for n, order in enumerate((p1_sb, p2_sb)):
                nc.vector.tensor_tensor(
                    both[:, n, :], val_win[t][:].indirect(order[:, list_cols]), weights[t, n, 0][:, first * BLOCK : (first + count) * BLOCK], ALU.mult
                )
            sources = (val_win[t][:, first * BLOCK : (first + count) * BLOCK], both[:, 0, :], both[:, 1, :])
            for k, source in enumerate(sources):
                for i in range(count):
                    nc.tensor.matmul(
                        nums[first + i][:, t * P : (t + 1) * P],
                        lhsT=source[:, i * BLOCK : (i + 1) * BLOCK],
                        rhs=ident[:],
                        is_transpose=True,
                        start=(k == 0),
                        stop=(k == len(sources) - 1),
                    )

        invs = []
        for b in range(BLOCKS):
            inv = keep.tile([P, 2, P, 2], F32, name=f"inv{b}", tag=f"inv{b}")
            nc.scalar.activation(
                out=inv[:],
                in_=den_sq[b][:].rearrange("j (u e p) -> j u p e", u=2, e=2),
                func=ACT.Abs_reciprocal_sqrt,
            )
            invs.append(inv)

        z_ts = []

        def normalise(b):
            z_t = ring.tile([P, 2, P, 2], BF16, name="z_t", align_bytes=64, bufs=4)
            nc.vector.tensor_tensor(
                z_t[:], nums[b][:].rearrange("j (u e p) -> j u p e", u=2, e=2), invs[b][:], ALU.mult
            )
            z_ts.append(z_t)

        w3_w = keep.tile([P, N], I32, name="w3_w", align_bytes=64)
        w3_s = keep.tile([P, N], U8, name="w3_s", align_bytes=64)
        deal_columns(nc, w3_s[:], w3_plane_raw[:])
        deal_columns(nc, w3_w[:], w3_raw[:])
        for t in range(PACK - 1):
            weighted_neighbours(t, 0, BLOCKS, f"c_win{PACK - 1 - t}")
        weighted_neighbours(PACK - 1, 0, 2, "c_win0")
        weighted_neighbours(PACK - 1, 1, 2, "last_terms")
        for b in range(BLOCKS):
            normalise(b)

        z_mx = []
        for b in range(BLOCKS):
            z_words = z_ts[b][:].rearrange("j u p e -> j (u p e)").bitcast(F32)
            back = psum.tile([P, 2, BLOCK], F32, name="prod", bufs=4)
            for u in range(2):
                nc.tensor.transpose(back[:, u, :], z_words[:, u * P : (u + 1) * P], ident[:])
            z = ring.tile([P, PACK * BLOCK], BF16, name="z", align_bytes=64, bufs=4)
            nc.scalar.copy(
                out=z[:].bitcast(F32).rearrange("p (j u) -> p j u", u=2), in_=back[:].rearrange("p u j -> p j u")
            )
            z_w = ring.tile([P, BLOCK], U32, name="z_w", align_bytes=64, bufs=4)
            z_s = ring.tile([P, BLOCK], U8, name="z_s", align_bytes=64, bufs=4)
            nc.vector.quantize_mx(out=z_w[:].bitcast(FP8X4), scales=z_s[:], in_=z[:])
            z_mx.append((z_w, z_s))

        ys = []
        for b in range(BLOCKS):
            cols = slice(b * BLOCK, (b + 1) * BLOCK)
            z_w, z_s = z_mx[b]
            y = ring.tile([P, PACK, BLOCK], F32, name="y", bufs=4)
            if b < BLOCKS - 1:
                y_bank = psum.tile([P, PACK, BLOCK], F32, name=f"y_bank{b}", tag=f"sum{b}", bufs=1)
                for t in range(PACK):
                    product(w3_w, w3_s, t, z_w[:], z_s[:], y_bank[:, t, :])
                nc.scalar.activation(out=y[:], in_=y_bank[:], func=ACT.Copy)
            else:
                low = psum.tile([P, 2, BLOCK], F32, name="y_low", tag=f"sum{b}", bufs=1)
                high = psum.tile([P, 2, BLOCK], F32, name="prod", bufs=4)
                for t in range(PACK):
                    product(w3_w, w3_s, t, z_w[:], z_s[:], (low, high)[t // 2][:, t % 2, :])
                nc.vector.tensor_copy(out=y[:, 0:2, :], in_=low[:])
                nc.scalar.activation(out=y[:, 2:4, :], in_=high[:], func=ACT.Copy)
            nc.sync.dma_start(out=out_rows[:, :, cols], in_=y[:])
            ys.append(y)

        for b in range(BLOCKS):
            cols = slice(b * BLOCK, (b + 1) * BLOCK)
            y_grouped = ring.tile([P, BLOCK, PACK], BF16, name="y_grouped", align_bytes=64, bufs=4)
            nc.vector.tensor_copy(out=y_grouped[:], in_=ys[b][:].rearrange("p t j -> p j t"))
            nc.vector.quantize_mx(
                out=y_words[:, cols].bitcast(FP8X4),
                scales=y_plane[:, cols],
                in_=y_grouped[:].rearrange("p j t -> p (j t)"),
            )
            if b >= BLOCKS - 2:
                done = slice(0, (b + 1) * BLOCK) if b == BLOCKS - 2 else cols
                nc.scalar.dma_start(out=out_words[:, done], in_=y_words[:, done].bitcast(I32))
        for q in range(4):
            queue = nc.sync if q % 2 == 0 else nc.scalar
            queue.dma_start(
                out=out_2[0, 4 * q : 4 * q + 4, :].bitcast(I32), in_=y_plane[32 * q : 32 * q + 4, :].bitcast(I32)
            )
